import numpy as np
import ml_dtypes


def mxq(x, axis, fmt="e4m3"):
    dtype, down = {"e4m3": (ml_dtypes.float8_e4m3fn, 7), "e5m2": (ml_dtypes.float8_e5m2, 14)}[fmt]
    v = np.moveaxis(np.asarray(x, np.float32).astype(ml_dtypes.bfloat16).astype(np.float64), axis, -1)
    blocks = v.reshape(v.shape[:-1] + (-1, 32))
    amax = np.abs(blocks).max(-1, keepdims=True)
    byte = np.maximum(np.where(amax > 0, np.frexp(amax)[1] - 1 + 127, 0) - down, 1)
    scale = np.exp2(byte - 127.0)
    codes = (blocks / scale).astype(np.float32).astype(dtype).astype(np.float64)
    return np.moveaxis((codes * scale).reshape(v.shape), -1, axis)


WIDE = False


def mx_kscale(k):
    if not WIDE:
        return np.ones(k)
    levels = np.array([10, -10, 5, -5, 0])
    if k % 512:
        return np.exp2(np.random.permutation(np.resize(levels, k // 32))).repeat(32)
    a = np.empty((k // 512, 16))
    for p in range(k // 512):
        a[p, :8] = np.random.permutation(np.resize(levels, 8))
        for g in range(8):
            far = levels[np.abs(levels - a[p, g]) >= 10]
            a[p, g + 8] = far[np.random.randint(len(far))]
    return np.exp2(a.ravel()).repeat(32)


def f64(x):
    return np.asarray(x).astype(np.float64)


def striped(idx):
    return np.tile(idx.reshape(-1, 16).T, (8, 1)).astype(np.uint16)


def unstriped(offs):
    return offs[:16].T.reshape(-1).astype(np.int64)


def striped8(idx):
    return np.concatenate([x.reshape(-1, 16).T for x in idx]).astype(np.uint16)


def runs(offs, k):
    lists = np.stack([offs[16 * r : 16 * r + 16].T.reshape(-1) for r in range(8)]).astype(np.int64)
    return lists[np.arange(k) % 512 // 64]


def pack_weight(w):
    k, n = w.shape
    w = f64(np.asarray(w, np.float32).astype(ml_dtypes.bfloat16)).reshape(k // 32, 32, n)
    amax = np.abs(w).max(1)
    byte = np.clip(np.where(amax > 0, np.frexp(amax)[1] - 1 + 127 - 7, 1), 1, 254)
    scaled = (w * np.exp2(127.0 - byte)[:, None, :]).reshape(k, n).astype(np.float32)
    words = np.ascontiguousarray(scaled.reshape(k // 512, 128, 4, n).transpose(0, 1, 3, 2)).astype(ml_dtypes.float8_e4m3fn).view(np.uint8)
    return words, np.ascontiguousarray(byte.astype(np.uint8).reshape(k // 512, 16, n))


def unpack_weight(words, scales):
    g, p, n, _ = words.shape
    vals = np.ascontiguousarray(words).view(ml_dtypes.float8_e4m3fn).astype(np.float64) * np.repeat(np.exp2(scales.astype(np.float64) - 127.0), 8, axis=1)[..., None]
    return vals.transpose(0, 1, 3, 2).reshape(g * 512, n)


def relu(v):
    return np.maximum(v, 0.0)


def sigmoid(v):
    return 1.0 / (1.0 + np.exp(-np.maximum(v, -700.0)))

def planes(y):
    n, m = y.shape
    v = y.astype(np.float32).astype(ml_dtypes.bfloat16).astype(np.float64).reshape(n // 32, 32, m)
    top = np.abs(v).max(1)
    byte = np.clip(np.where(top > 0, np.frexp(top)[1] - 1 + 127 - 7, 1), 1, 254)
    codes = (v * np.exp2(127.0 - byte)[:, None, :]).reshape(n, m).astype(np.float32).astype(ml_dtypes.float8_e4m3fn).view(np.uint8)
    words = codes.reshape(n // 512, 128, 4, m).transpose(0, 1, 3, 2)
    return np.ascontiguousarray(words), np.ascontiguousarray(byte.astype(np.uint8).reshape(n // 512, 16, m))


K, T, S, V, H = 512, 2048, 512, 512, 512


def setup_inputs():
    n = np.random.standard_normal
    s = mx_kscale(K)[:, None]
    u = mx_kscale(S)
    packed_xT = pack_weight(n((K, T)) * s)
    packed_w1 = pack_weight(n((K, H)) / np.sqrt(K) / s)
    packed_w2 = pack_weight(n((K, H)) / np.sqrt(K) / s)
    return {
        "x_words": packed_xT[0],
        "x_scales": packed_xT[1],
        "w1_words": packed_w1[0],
        "w1_scales": packed_w1[1],
        "w2_words": packed_w2[0],
        "w2_scales": packed_w2[1],
        "ga": (np.random.uniform(0.5, 1.5, (H, 1)) * u[:, None]).astype(np.float32),
        "gb": (np.random.uniform(0.5, 1.5, (H, 1)) / u[:, None]).astype(np.float32),
        "offs": striped(np.random.permutation(T)[:S]),
        "two": striped(np.random.permutation(T)[:V]),
        "n1": striped8(np.stack([np.random.permutation(S) for _ in range(8)])),
        "n2": striped8(np.stack([np.random.permutation(S) for _ in range(8)])),
        "n3": striped8(np.stack([np.random.permutation(V) for _ in range(8)])),
        "n4": striped8(np.stack([np.random.permutation(V) for _ in range(8)])),
        "n5": striped8(np.stack([np.random.permutation(V) for _ in range(8)])),
        "n6": striped8(np.stack([np.random.permutation(V) for _ in range(8)])),
        "n7": striped8(np.stack([np.random.permutation(V) for _ in range(8)])),
    }


def reference(x_words, x_scales, w1_words, w1_scales, w2_words, w2_scales, ga, gb, offs, two, n1, n2, n3, n4, n5, n6, n7):
    xq = unpack_weight(x_words, x_scales)[:, unstriped(offs)]
    a = unpack_weight(w1_words, w1_scales).T @ xq
    pa = a - (a[np.arange(H)[:, None], runs(n1, H)])
    pb = a[np.arange(H)[:, None], runs(n2, H)] - a
    z = f64(ga) * (relu(np.minimum(pa, pb)) - (relu(-1.0 * np.maximum(pa, pb))))
    x_two = unpack_weight(x_words, x_scales)[:, unstriped(two)]
    b = unpack_weight(w2_words, w2_scales).T @ x_two
    pa2 = b[np.arange(H)[:, None], runs(n3, H)]
    z2 = f64(gb) * (pa2 + (sigmoid(b[np.arange(H)[:, None], runs(n4, H)])) * (b[np.arange(H)[:, None], runs(n5, H)] - pa2))
    s = 0.0625 * ((mxq(z, 0, "e4m3").T @ mxq(z2, 0, "e4m3")))
    st = s * (sigmoid(s[np.arange(S)[:, None], runs(n6, S)]))
    out_0 = st - (st[np.arange(S)[:, None], runs(n7, S)])
    return (out_0,) + planes(out_0)

@@ -1,0 +1,285 @@
+from contextlib import ExitStack
+
+import concourse.mybir as mybir
+
+F32 = mybir.dt.float32
+BF16 = mybir.dt.bfloat16
+I32 = mybir.dt.int32
+U32 = mybir.dt.uint32
+U16 = mybir.dt.uint16
+U8 = mybir.dt.uint8
+FP8X4 = mybir.dt.float8_e4m3fn_x4
+ALU = mybir.AluOpType
+ACT = mybir.ActivationFunctionType
+
+P = 128
+PACK = 4
+T = 2048
+N = 512
+HALF = N // 2
+LIST_COLS = N // 16
+WIDE = 2 * N
+S_SCALE = 0.0625
+
+FLOPS = 3 * 2 * 512 * 512 * 512
+
+
+def tile_picked_kqminmodlerphopg_none_po_kernel(
+    tc, x_words, x_scales, w1_words, w1_scales, w2_words, w2_scales, ga, gb,
+    offs, two, n1, n2, n3, n4, n5, n6, n7, out_0, out_1, out_2,
+):
+    nc = tc.nc
+    halves = [slice(0, HALF), slice(HALF, N)]
+    list_halves = [slice(0, LIST_COLS // 2), slice(LIST_COLS // 2, LIST_COLS)]
+
+    with ExitStack() as ctx:
+        held = ctx.enter_context(tc.tile_pool(name="held", bufs=1))
+        ring = ctx.enter_context(tc.tile_pool(name="ring", bufs=2))
+        psum = ctx.enter_context(tc.psum_pool(name="psum", bufs=1))
+
+        def new(name, shape, dtype):
+            return held.tile(shape, dtype, name=name, align_bytes=64)
+
+        def load_list(name, src):
+            tile = held.tile([P, LIST_COLS], U16, name=name)
+            nc.sync.dma_start(tile[:], src)
+            return tile
+
+        def zeroed_scale_tile(name, width):
+            tile = new(name, [P, width], U8)
+            nc.vector.memset(tile[:].bitcast(I32), 0)
+            return tile
+
+        def load_scales(tile, src):
+            for q in range(4):
+                nc.sync.dma_start(
+                    tile[32 * q : 32 * q + 4, :].bitcast(I32), src[0, 4 * q : 4 * q + 4, :].bitcast(I32)
+                )
+
+        def load_words(name, src, width):
+            tile = new(name, [P, width], U32)
+            nc.sync.dma_start(tile[:].bitcast(I32), src[0].rearrange("p n t -> p (n t)").bitcast(I32))
+            return tile
+
+        def load_gain(name, src):
+            tile = new(name, [P, PACK], F32)
+            nc.sync.dma_start(tile[:], src.rearrange("(p t) o -> p (t o)", t=PACK))
+            return tile
+
+        x_sc = zeroed_scale_tile("x_sc", T)
+        w1_sc = zeroed_scale_tile("w1_sc", N)
+        w2_sc = zeroed_scale_tile("w2_sc", N)
+
+        l_offs = load_list("l_offs", offs)
+        load_scales(x_sc, x_scales)
+        l_two = load_list("l_two", two)
+        x_w = load_words("x_w", x_words, T)
+        w1_w = load_words("w1_w", w1_words, N)
+        load_scales(w1_sc, w1_scales)
+        ga_t = load_gain("ga_t", ga)
+        l_n1 = load_list("l_n1", n1)
+        l_n2 = load_list("l_n2", n2)
+        w2_w = load_words("w2_w", w2_words, N)
+        load_scales(w2_sc, w2_scales)
+        gb_t = load_gain("gb_t", gb)
+        l_n4 = load_list("l_n4", n4)
+        l_n5 = load_list("l_n5", n5)
+        l_n3 = load_list("l_n3", n3)
+        l_n6 = load_list("l_n6", n6)
+        l_n7 = load_list("l_n7", n7)
+
+        pos_win = [new("pos_win%d" % t, [P, WIDE], F32) for t in range(PACK)]
+        neg_win = [new("neg_win%d" % t, [P, WIDE], F32) for t in range(PACK)]
+        for t in range(PACK):
+            nc.vector.memset(pos_win[t][:, N:], 0.0)
+            nc.scalar.activation(neg_win[t][:, N:], pos_win[t][:, N:], ACT.Sigmoid)
+
+        def pick(name, window, offsets, dtype):
+            tile = new(name, [P, N], dtype)
+            nc.vector.tensor_copy(tile[:], window[:].indirect(offsets[:]))
+            return tile
+
+        def deal(name, words, scales):
+            dealt_w = new(name + "_dw", [P, N], U32)
+            dealt_s = new(name + "_ds", [P, N], U8)
+            nc.vector.tensor_copy(
+                dealt_w[:].bitcast(I32).rearrange("p (t c i) -> p c t i", t=PACK, i=4),
+                words[:].bitcast(I32).rearrange("p (c i t) -> p c t i", t=PACK, i=4),
+            )
+            nc.vector.tensor_copy(
+                dealt_s[:].rearrange("p (t c i) -> p c t i", t=PACK, i=16),
+                scales[:].rearrange("p (c i t) -> p c t i", t=PACK, i=16),
+            )
+            return dealt_w, dealt_s
+
+        def product(bank, lhs_w, lhs_s, t, rhs_w, rhs_s):
+            cols = slice(P * t, P * (t + 1))
+            nc.tensor.matmul_mx(
+                out=bank, lhsT=lhs_w[:, cols].bitcast(FP8X4), lhsT_scale=lhs_s[:, cols],
+                rhs=rhs_w.bitcast(FP8X4), rhs_scale=rhs_s, start=True, stop=True,
+            )
+
+        xa_s = pick("xa_s", x_sc, l_offs, U8)
+        xb_s = pick("xb_s", x_sc, l_two, U8)
+        w1_dw, w1_ds = deal("w1", w1_w, w1_sc)
+        xa_w = pick("xa_w", x_w, l_offs, U32)
+        xb_w = pick("xb_w", x_w, l_two, U32)
+        w2_dw, w2_ds = deal("w2", w2_w, w2_sc)
+
+        a_bank = [psum.tile([P, N], F32, name="a_bank%d" % t) for t in range(PACK)]
+        b_bank = [psum.tile([P, N], F32, name="b_bank%d" % t) for t in range(PACK)]
+        for t in range(PACK):
+            product(a_bank[t][:], w1_dw, w1_ds, t, xa_w[:], xa_s[:])
+        for t in range(PACK):
+            product(b_bank[t][:], w2_dw, w2_ds, t, xb_w[:], xb_s[:])
+
+        neg_gb = new("neg_gb", [P, PACK], F32)
+        nc.gpsimd.tensor_scalar(neg_gb[:], gb_t[:], -1.0, 0.0, ALU.mult, ALU.add)
+
+        for t in range(PACK):
+            nc.scalar.activation(pos_win[t][:, :N], a_bank[t][:], ACT.Copy, scale=ga_t[:, t : t + 1])
+            nc.scalar.activation(neg_win[t][:, :N], pos_win[t][:, :N], ACT.Copy, scale=-1.0)
+        b_win = [new("b_win%d" % t, [P, N], F32) for t in range(PACK)]
+        sig = [[new("sig%d%d" % (h, t), [P, HALF], F32) for t in range(PACK)] for h in range(2)]
+        rest = [[new("rest%d%d" % (h, t), [P, HALF], F32) for t in range(PACK)] for h in range(2)]
+        for t in range(PACK):
+            nc.scalar.copy(b_win[t][:], b_bank[t][:])
+        for h in range(2):
+            for t in range(PACK):
+                nc.scalar.activation(sig[h][t][:], b_win[t][:].indirect(l_n4[:, list_halves[h]]), ACT.Sigmoid)
+                nc.scalar.activation(
+                    rest[h][t][:], sig[h][t][:], ACT.Identity,
+                    scale=neg_gb[:, t : t + 1], bias=gb_t[:, t : t + 1],
+                )
+
+        z_rows = new("z_rows", [P, PACK, N], BF16)
+        pa, pb, low = {}, {}, {}
+        for t in range(PACK + 1):
+            if t < PACK:
+                pa[t] = ring.tile([P, N], F32, name="pa")
+                nc.vector.tensor_tensor(pa[t][:], neg_win[t][:].indirect(l_n1[:]), pos_win[t][:, :N], ALU.add)
+            if t > 0:
+                low[t - 1] = ring.tile([P, N], F32, name="low")
+                nc.vector.scalar_tensor_tensor(low[t - 1][:], pa[t - 1][:], 0.0, pb[t - 1][:], ALU.min, ALU.max)
+            if t < PACK:
+                pb[t] = ring.tile([P, N], F32, name="pb")
+                nc.vector.tensor_tensor(pb[t][:], pos_win[t][:].indirect(l_n2[:]), neg_win[t][:, :N], ALU.add)
+            if t > 0:
+                nc.vector.scalar_tensor_tensor(z_rows[:, t - 1, :], pa[t - 1][:], 0.0, low[t - 1][:], ALU.max, ALU.min)
+
+        z_in = new("z_in", [P, PACK * N], BF16)
+        nc.scalar.copy(
+            z_in[:].rearrange("p (u c i t) -> p c t i u", u=PACK, i=2, t=PACK),
+            z_rows[:].rearrange("p t (c i u) -> p c t i u", i=2, u=PACK),
+        )
+        z_w = new("z_w", [P, N], U32)
+        z_s = new("z_s", [P, N], U8)
+
+        def weave(engine_copy, dst, src):
+            engine_copy(
+                dst[:].rearrange("p (c i t) -> p c t i", i=4, t=PACK),
+                src[:].rearrange("p t (c i) -> p c t i", i=4),
+            )
+
+        neg_s0 = new("neg_s0", [P, N], F32)
+        for h in range(2):
+            z2_rows = new("z2_rows%d" % h, [P, PACK, HALF], BF16)
+            far, near = {}, {}
+            for t in range(PACK + 1):
+                if t < PACK:
+                    far[t] = ring.tile([P, HALF], F32, name="far")
+                    nc.vector.tensor_tensor(
+                        far[t][:], b_win[t][:].indirect(l_n5[:, list_halves[h]]), sig[h][t][:], ALU.mult)
+                if t > 0:
+                    nc.vector.scalar_tensor_tensor(
+                        z2_rows[:, t - 1, :], far[t - 1][:], gb_t[:, t - 1 : t], near[t - 1][:], ALU.mult, ALU.add)
+                if t < PACK:
+                    near[t] = ring.tile([P, HALF], F32, name="near")
+                    nc.vector.tensor_tensor(
+                        near[t][:], b_win[t][:].indirect(l_n3[:, list_halves[h]]), rest[h][t][:], ALU.mult)
+                if h == 1 and t == 0:
+                    nc.vector.quantize_mx(z_w[:].bitcast(FP8X4), z_s[:], z_in[:])
+                if h == 1 and t == 1:
+                    nc.vector.quantize_mx(z2_w[:].bitcast(FP8X4), z2_s[:], z2_in[:])
+                    for u in range(PACK):
+                        product(a_bank[u][:, halves[0]], z_w, z_s, u, z2_w[:], z2_s[:])
+                    nc.scalar.activation(pos_win[0][:, halves[0]], a_bank[0][:, halves[0]], ACT.Sigmoid, scale=S_SCALE)
+                    nc.scalar.activation(neg_s0[:, halves[0]], a_bank[0][:, halves[0]], ACT.Copy, scale=-S_SCALE)
+                    for u in range(1, PACK):
+                        nc.scalar.activation(pos_win[u][:, halves[0]], a_bank[u][:, halves[0]], ACT.Copy, scale=S_SCALE)
+            z2_in = new("z2_in%d" % h, [P, PACK * HALF], BF16)
+            z2_w = new("z2_w%d" % h, [P, HALF], U32)
+            z2_s = new("z2_s%d" % h, [P, HALF], U8)
+            weave(nc.scalar.copy if h == 0 else nc.vector.tensor_copy, z2_in, z2_rows)
+
+        nc.vector.quantize_mx(z2_w[:].bitcast(FP8X4), z2_s[:], z2_in[:])
+        for u in range(PACK):
+            product(a_bank[u][:, halves[1]], z_w, z_s, u, z2_w[:], z2_s[:])
+
+        gate = [None] + [new("gate%d" % u, [P, N], F32) for u in range(1, PACK)]
+        st = [new("st%d" % u, [P, N], F32) for u in range(PACK)]
+        res = [new("res%d" % h, [P, PACK, HALF], F32) for h in range(2)]
+        out_rows = out_0.rearrange("(p u) v -> p u v", u=PACK)
+
+        def s_copy(u):
+            nc.scalar.activation(pos_win[u][:, halves[1]], a_bank[u][:, halves[1]], ACT.Copy, scale=S_SCALE)
+
+        def gate_gather(u):
+            nc.scalar.activation(gate[u][:], pos_win[u][:].indirect(l_n6[:]), ACT.Sigmoid)
+
+        def neg_st(u):
+            nc.vector.scalar_tensor_tensor(neg_win[u][:, :N], a_bank[u][:], -S_SCALE, gate[u][:], ALU.mult, ALU.mult)
+
+        def flip(u):
+            nc.scalar.activation(st[u][:], neg_win[u][:, :N], ACT.Copy, scale=-1.0)
+
+        def hop(u, h):
+            nc.vector.tensor_tensor(
+                res[h][:, u, :], neg_win[u][:].indirect(l_n7[:, list_halves[h]]), st[u][:, halves[h]], ALU.add)
+
+        def store(h, us):
+            nc.sync.dma_start(out_rows[:, us, halves[h]], res[h][:, us, :])
+
+        nc.scalar.activation(pos_win[0][:, halves[1]], a_bank[0][:, halves[1]], ACT.Sigmoid, scale=S_SCALE)
+        nc.vector.tensor_scalar(pos_win[1][:, halves[1]], a_bank[1][:, halves[1]], S_SCALE, None, ALU.mult)
+        nc.vector.tensor_scalar(neg_s0[:, halves[1]], a_bank[0][:, halves[1]], -S_SCALE, None, ALU.mult)
+        gate_gather(1)
+        nc.vector.tensor_tensor(neg_win[0][:, :N], pos_win[0][:].indirect(l_n6[:]), neg_s0[:], ALU.mult)
+        s_copy(2)
+        flip(0)
+        neg_st(1)
+        gate_gather(2)
+        hop(0, 0)
+        hop(0, 1)
+        flip(1)
+        s_copy(3)
+        neg_st(2)
+        gate_gather(3)
+        hop(1, 0)
+        hop(1, 1)
+        store(0, slice(0, 2))
+        store(1, slice(0, 2))
+        flip(2)
+        neg_st(3)
+        flip(3)
+        hop(2, 0)
+        hop(3, 0)
+        store(0, slice(2, 4))
+        y_in = [new("y_in%d" % h, [P, PACK * HALF], BF16) for h in range(2)]
+        y_w = [new("y_w%d" % h, [P, HALF], U32) for h in range(2)]
+        y_s = new("y_s", [P, N], U8)
+        weave(nc.scalar.copy, y_in[0], res[0])
+        hop(2, 1)
+        store(1, slice(2, 3))
+        hop(3, 1)
+        store(1, slice(3, 4))
+        weave(nc.vector.tensor_copy, y_in[1], res[1])
+        words_out = out_1[0].rearrange("p n t -> p (n t)").bitcast(I32)
+        for h in range(2):
+            nc.vector.quantize_mx(y_w[h][:].bitcast(FP8X4), y_s[:, halves[h]], y_in[h][:])
+            nc.sync.dma_start(words_out[:, halves[h]], y_w[h][:].bitcast(I32))
+        for q in range(4):
+            queue = nc.scalar if q % 2 else nc.sync
+            queue.dma_start(
+                out_2[0, 4 * q : 4 * q + 4, :].bitcast(I32), y_s[32 * q : 32 * q + 4, :].bitcast(I32)
+            )

@@ -1,6 +1,7 @@
 from contextlib import ExitStack
 
 import concourse.mybir as mybir
+from concourse.masks import make_identity
 
 F32 = mybir.dt.float32
 BF16 = mybir.dt.bfloat16
@@ -20,6 +21,7 @@ HALF = N // 2
 LIST_COLS = N // 16
 WIDE = 2 * N
 S_SCALE = 0.0625
+VECTOR_COLS = 160
 
 FLOPS = 3 * 2 * 512 * 512 * 512
 
@@ -45,15 +47,10 @@ def tile_picked_kqminmodlerphopg_none_po_kernel(
             nc.sync.dma_start(tile[:], src)
             return tile
 
-        def zeroed_scale_tile(name, width):
-            tile = new(name, [P, width], U8)
-            nc.vector.memset(tile[:].bitcast(I32), 0)
-            return tile
-
-        def load_scales(tile, src):
+        def load_scales(queues, tile, first, src):
             for q in range(4):
-                nc.sync.dma_start(
-                    tile[32 * q : 32 * q + 4, :].bitcast(I32), src[0, 4 * q : 4 * q + 4, :].bitcast(I32)
+                queues[q].dma_start(
+                    tile[32 * q + first : 32 * q + first + 4, :].bitcast(I32), src[0, 4 * q : 4 * q + 4, :].bitcast(I32)
                 )
 
         def load_words(name, src, width):
@@ -63,25 +60,28 @@ def tile_picked_kqminmodlerphopg_none_po_kernel(
 
         def load_gain(name, src):
             tile = new(name, [P, PACK], F32)
-            nc.sync.dma_start(tile[:], src.rearrange("(p t) o -> p (t o)", t=PACK))
-            return tile
+            negated = new("neg_" + name, [P, PACK], F32)
+            nc.gpsimd.dma_start(tile[:], src.rearrange("(p t) o -> p (t o)", t=PACK))
+            nc.gpsimd.tensor_scalar(negated[:], tile[:], -1.0, 0.0, ALU.mult, ALU.add)
+            return tile, negated
 
-        x_sc = zeroed_scale_tile("x_sc", T)
-        w1_sc = zeroed_scale_tile("w1_sc", N)
-        w2_sc = zeroed_scale_tile("w2_sc", N)
+        x_sc = new("x_sc", [P, T], U8)
+        w_sc = held.tile([P, N], U8, name="w_sc", tag="w_sc_then_xb_w", align_bytes=64)
+        nc.gpsimd.memset(x_sc[:].bitcast(I32), 0)
+        nc.gpsimd.memset(w_sc[:].bitcast(I32), 0)
 
+        w1_w = load_words("w1_w", w1_words, N)
         l_offs = load_list("l_offs", offs)
-        load_scales(x_sc, x_scales)
+        load_scales([nc.sync] * 4, x_sc, 0, x_scales)
         l_two = load_list("l_two", two)
         x_w = load_words("x_w", x_words, T)
-        w1_w = load_words("w1_w", w1_words, N)
-        load_scales(w1_sc, w1_scales)
-        ga_t = load_gain("ga_t", ga)
+        load_scales([nc.sync] * 4, w_sc, 0, w1_scales)
+        load_scales([nc.sync] * 3 + [nc.gpsimd], w_sc, 4, w2_scales)
+        ga_t, neg_ga = load_gain("ga_t", ga)
         l_n1 = load_list("l_n1", n1)
         l_n2 = load_list("l_n2", n2)
         w2_w = load_words("w2_w", w2_words, N)
-        load_scales(w2_sc, w2_scales)
-        gb_t = load_gain("gb_t", gb)
+        gb_t, neg_gb = load_gain("gb_t", gb)
         l_n4 = load_list("l_n4", n4)
         l_n5 = load_list("l_n5", n5)
         l_n3 = load_list("l_n3", n3)
@@ -94,78 +94,88 @@ def tile_picked_kqminmodlerphopg_none_po_kernel(
             nc.vector.memset(pos_win[t][:, N:], 0.0)
             nc.scalar.activation(neg_win[t][:, N:], pos_win[t][:, N:], ACT.Sigmoid)
 
-        def pick(name, window, offsets, dtype):
-            tile = new(name, [P, N], dtype)
+        ident = new("ident", [P, P], F32)
+        make_identity(nc, ident[:])
+
+        def pick(tile, window, offsets):
             nc.vector.tensor_copy(tile[:], window[:].indirect(offsets[:]))
             return tile
 
-        def deal(name, words, scales):
-            dealt_w = new(name + "_dw", [P, N], U32)
-            dealt_s = new(name + "_ds", [P, N], U8)
+        def deal(name, src, dtype, run):
+            dealt = new(name, [P, N], src.dtype)
             nc.vector.tensor_copy(
-                dealt_w[:].bitcast(I32).rearrange("p (t c i) -> p c t i", t=PACK, i=4),
-                words[:].bitcast(I32).rearrange("p (c i t) -> p c t i", t=PACK, i=4),
+                dealt[:].bitcast(dtype).rearrange("p (t c i) -> p c t i", t=PACK, i=run),
+                src[:].bitcast(dtype).rearrange("p (c i t) -> p c t i", t=PACK, i=run),
             )
-            nc.vector.tensor_copy(
-                dealt_s[:].rearrange("p (t c i) -> p c t i", t=PACK, i=16),
-                scales[:].rearrange("p (c i t) -> p c t i", t=PACK, i=16),
-            )
-            return dealt_w, dealt_s
+            return dealt
 
-        def product(bank, lhs_w, lhs_s, t, rhs_w, rhs_s):
+        def product(bank, lhs_w, lhs_s, t, rhs_w, rhs_s, first=0):
             cols = slice(P * t, P * (t + 1))
             nc.tensor.matmul_mx(
-                out=bank, lhsT=lhs_w[:, cols].bitcast(FP8X4), lhsT_scale=lhs_s[:, cols],
+                out=bank, lhsT=lhs_w[:, cols].bitcast(FP8X4), lhsT_scale=lhs_s[first:, cols],
                 rhs=rhs_w.bitcast(FP8X4), rhs_scale=rhs_s, start=True, stop=True,
             )
 
-        xa_s = pick("xa_s", x_sc, l_offs, U8)
-        xb_s = pick("xb_s", x_sc, l_two, U8)
-        w1_dw, w1_ds = deal("w1", w1_w, w1_sc)
-        xa_w = pick("xa_w", x_w, l_offs, U32)
-        xb_w = pick("xb_w", x_w, l_two, U32)
-        w2_dw, w2_ds = deal("w2", w2_w, w2_sc)
+        w1_dw = deal("w1_dw", w1_w, I32, 4)
+        xa_s = pick(new("xa_s", [P, N], U8), x_sc, l_offs)
+        xb_s = pick(new("xb_s", [P, N], U8), x_sc, l_two)
+        xa_w = pick(new("xa_w", [P, N], U32), x_w, l_offs)
+        w_ds = deal("w_ds", w_sc, U8, 16)
+        xb_w = pick(held.tile([P, N], U32, name="xb_w", tag="w_sc_then_xb_w", align_bytes=64), x_w, l_two)
+        w2_dw = deal("w2_dw", w2_w, I32, 4)
 
         a_bank = [psum.tile([P, N], F32, name="a_bank%d" % t) for t in range(PACK)]
         b_bank = [psum.tile([P, N], F32, name="b_bank%d" % t) for t in range(PACK)]
         for t in range(PACK):
-            product(a_bank[t][:], w1_dw, w1_ds, t, xa_w[:], xa_s[:])
+            product(a_bank[t][:], w1_dw, w_ds, t, xa_w[:], xa_s[:])
         for t in range(PACK):
-            product(b_bank[t][:], w2_dw, w2_ds, t, xb_w[:], xb_s[:])
+            product(b_bank[t][:], w2_dw, w_ds, t, xb_w[:], xb_s[:], first=4)
 
-        neg_gb = new("neg_gb", [P, PACK], F32)
-        nc.gpsimd.tensor_scalar(neg_gb[:], gb_t[:], -1.0, 0.0, ALU.mult, ALU.add)
 
         for t in range(PACK):
             nc.scalar.activation(pos_win[t][:, :N], a_bank[t][:], ACT.Copy, scale=ga_t[:, t : t + 1])
-            nc.scalar.activation(neg_win[t][:, :N], pos_win[t][:, :N], ACT.Copy, scale=-1.0)
+            nc.scalar.activation(neg_win[t][:, :N], a_bank[t][:], ACT.Copy, scale=neg_ga[:, t : t + 1])
         b_win = [new("b_win%d" % t, [P, N], F32) for t in range(PACK)]
         sig = [[new("sig%d%d" % (h, t), [P, HALF], F32) for t in range(PACK)] for h in range(2)]
         rest = [[new("rest%d%d" % (h, t), [P, HALF], F32) for t in range(PACK)] for h in range(2)]
-        for t in range(PACK):
+
+        def b_copy(t):
             nc.scalar.copy(b_win[t][:], b_bank[t][:])
-        for h in range(2):
-            for t in range(PACK):
-                nc.scalar.activation(sig[h][t][:], b_win[t][:].indirect(l_n4[:, list_halves[h]]), ACT.Sigmoid)
-                nc.scalar.activation(
-                    rest[h][t][:], sig[h][t][:], ACT.Identity,
-                    scale=neg_gb[:, t : t + 1], bias=gb_t[:, t : t + 1],
-                )
+
+        def mix_weights(h, t):
+            nc.scalar.activation(sig[h][t][:], b_win[t][:].indirect(l_n4[:, list_halves[h]]), ACT.Sigmoid)
+            nc.scalar.activation(
+                rest[h][t][:], sig[h][t][:], ACT.Identity,
+                scale=neg_gb[:, t : t + 1], bias=gb_t[:, t : t + 1],
+            )
+            if h == 0:
+                nc.scalar.activation(sig[h][t][:], sig[h][t][:], ACT.Copy, scale=gb_t[:, t : t + 1])
+
+        between = [
+            [lambda: b_copy(0)],
+            [lambda: b_copy(1), lambda: b_copy(2), lambda: b_copy(3), lambda: mix_weights(0, 0)],
+            [lambda: mix_weights(0, 1), lambda: mix_weights(0, 2), lambda: mix_weights(0, 3)],
+            [lambda: mix_weights(1, 0), lambda: mix_weights(1, 1), lambda: mix_weights(1, 2), lambda: mix_weights(1, 3)],
+        ]
 
         z_rows = new("z_rows", [P, PACK, N], BF16)
-        pa, pb, low = {}, {}, {}
+        pa, pb, low, high = {}, {}, {}, {}
         for t in range(PACK + 1):
             if t < PACK:
                 pa[t] = ring.tile([P, N], F32, name="pa")
                 nc.vector.tensor_tensor(pa[t][:], neg_win[t][:].indirect(l_n1[:]), pos_win[t][:, :N], ALU.add)
+                high[t] = ring.tile([P, N], BF16, name="high")
+                nc.scalar.activation(high[t][:], pa[t][:], ACT.Relu)
+                for step in between[t]:
+                    step()
             if t > 0:
-                low[t - 1] = ring.tile([P, N], F32, name="low")
+                low[t - 1] = ring.tile([P, N], BF16, name="low")
                 nc.vector.scalar_tensor_tensor(low[t - 1][:], pa[t - 1][:], 0.0, pb[t - 1][:], ALU.min, ALU.max)
             if t < PACK:
                 pb[t] = ring.tile([P, N], F32, name="pb")
                 nc.vector.tensor_tensor(pb[t][:], pos_win[t][:].indirect(l_n2[:]), neg_win[t][:, :N], ALU.add)
             if t > 0:
-                nc.vector.scalar_tensor_tensor(z_rows[:, t - 1, :], pa[t - 1][:], 0.0, low[t - 1][:], ALU.max, ALU.min)
+                nc.vector.tensor_tensor(z_rows[:, t - 1, :], high[t - 1][:], low[t - 1][:], ALU.min)
 
         z_in = new("z_in", [P, PACK * N], BF16)
         nc.scalar.copy(
@@ -175,46 +185,89 @@ def tile_picked_kqminmodlerphopg_none_po_kernel(
         z_w = new("z_w", [P, N], U32)
         z_s = new("z_s", [P, N], U8)
 
-        def weave(engine_copy, dst, src):
-            engine_copy(
-                dst[:].rearrange("p (c i t) -> p c t i", i=4, t=PACK),
-                src[:].rearrange("p t (c i) -> p c t i", i=4),
+        def weave_scalar(dst, src, cols):
+            nc.scalar.copy(
+                dst[:].rearrange("p (c t) -> p c t", t=PACK)[:, cols, :].rearrange("p (c i) t -> p c t i", i=4),
+                src[:, :, cols].rearrange("p t (c i) -> p c t i", i=4),
             )
 
-        neg_s0 = new("neg_s0", [P, N], F32)
-        for h in range(2):
-            z2_rows = new("z2_rows%d" % h, [P, PACK, HALF], BF16)
-            far, near = {}, {}
-            for t in range(PACK + 1):
-                if t < PACK:
-                    far[t] = ring.tile([P, HALF], F32, name="far")
-                    nc.vector.tensor_tensor(
-                        far[t][:], b_win[t][:].indirect(l_n5[:, list_halves[h]]), sig[h][t][:], ALU.mult)
-                if t > 0:
-                    nc.vector.scalar_tensor_tensor(
-                        z2_rows[:, t - 1, :], far[t - 1][:], gb_t[:, t - 1 : t], near[t - 1][:], ALU.mult, ALU.add)
-                if t < PACK:
-                    near[t] = ring.tile([P, HALF], F32, name="near")
-                    nc.vector.tensor_tensor(
-                        near[t][:], b_win[t][:].indirect(l_n3[:, list_halves[h]]), rest[h][t][:], ALU.mult)
-                if h == 1 and t == 0:
-                    nc.vector.quantize_mx(z_w[:].bitcast(FP8X4), z_s[:], z_in[:])
-                if h == 1 and t == 1:
-                    nc.vector.quantize_mx(z2_w[:].bitcast(FP8X4), z2_s[:], z2_in[:])
-                    for u in range(PACK):
-                        product(a_bank[u][:, halves[0]], z_w, z_s, u, z2_w[:], z2_s[:])
-                    nc.scalar.activation(pos_win[0][:, halves[0]], a_bank[0][:, halves[0]], ACT.Sigmoid, scale=S_SCALE)
-                    nc.scalar.activation(neg_s0[:, halves[0]], a_bank[0][:, halves[0]], ACT.Copy, scale=-S_SCALE)
-                    for u in range(1, PACK):
-                        nc.scalar.activation(pos_win[u][:, halves[0]], a_bank[u][:, halves[0]], ACT.Copy, scale=S_SCALE)
-            z2_in = new("z2_in%d" % h, [P, PACK * HALF], BF16)
-            z2_w = new("z2_w%d" % h, [P, HALF], U32)
-            z2_s = new("z2_s%d" % h, [P, HALF], U8)
-            weave(nc.scalar.copy if h == 0 else nc.vector.tensor_copy, z2_in, z2_rows)
+        def weave_shared(dst, src):
+            cols = slice(0, VECTOR_COLS)
+            nc.vector.tensor_copy(
+                dst[:].rearrange("p (c t) -> p c t", t=PACK)[:, cols, :], src[:, :, cols].rearrange("p t c -> p c t")
+            )
+            weave_scalar(dst, src, slice(VECTOR_COLS, HALF))
 
-        nc.vector.quantize_mx(z2_w[:].bitcast(FP8X4), z2_s[:], z2_in[:])
+        neg_s0 = new("neg_s0", [P, N], F32)
+        z2_in = [
+            held.tile([P, PACK * HALF], BF16, name="z2_in0", tag="z2_in0_then_far", align_bytes=64),
+            new("z2_in1", [P, PACK * HALF], BF16),
+        ]
+        z2_w = [new("z2_w%d" % h, [P, HALF], U32) for h in range(2)]
+        z2_s = [new("z2_s%d" % h, [P, HALF], U8) for h in range(2)]
+
+        def far_term(h, t):
+            if (h, t) == (1, PACK - 1):
+                far = held.tile([P, HALF], F32, name="last_far", tag="z2_in0_then_far", align_bytes=64)
+            else:
+                far = ring.tile([P, HALF], F32, name="far")
+            nc.vector.tensor_tensor(far[:], b_win[t][:].indirect(l_n5[:, list_halves[h]]), sig[h][t][:], ALU.mult)
+            return far
+
+        def near_term(h, t):
+            near = ring.tile([P, HALF], F32, name="near")
+            nc.vector.tensor_tensor(near[:], b_win[t][:].indirect(l_n3[:, list_halves[h]]), rest[h][t][:], ALU.mult)
+            return near
+
+        def quantize(codes, scales, values):
+            nc.vector.quantize_mx(codes.bitcast(FP8X4), scales, values)
+
+        def block(k):
+            return slice(P * k, P * (k + 1))
+
+        sum_bank, word_bank = b_bank[:2], b_bank[2]
+        for t in range(PACK):
+            far, near = far_term(0, t), near_term(0, t)
+            for k in range(2):
+                nc.tensor.matmul(sum_bank[k][:, block(t)], far[:, block(k)], ident[:], start=True, stop=False, is_transpose=True)
+                nc.tensor.matmul(sum_bank[k][:, block(t)], near[:, block(k)], ident[:], start=False, stop=True, is_transpose=True)
+        for k in range(2):
+            turned = new("turned%d" % k, [P, N], BF16)
+            nc.scalar.copy(
+                turned[:].rearrange("v (u p s) -> v u p s", u=2, s=2),
+                sum_bank[k][:].rearrange("v (u s p) -> v u p s", u=2, s=2),
+            )
+            for u in range(2):
+                nc.tensor.transpose(word_bank[:, block(2 * k + u)], turned[:].bitcast(F32)[:, block(u)], ident[:])
+        nc.scalar.copy(
+            z2_in[0][:].bitcast(F32).rearrange("p (k v u) -> p k v u", k=2, u=2),
+            word_bank[:].rearrange("p (k u v) -> p k v u", k=2, u=2),
+        )
+
+        z2_rows = new("z2_rows", [P, PACK, HALF], BF16)
+        far, near = {}, {}
+        for t in range(PACK + 1):
+            if t < PACK:
+                far[t] = far_term(1, t)
+            if t > 0:
+                nc.vector.scalar_tensor_tensor(
+                    z2_rows[:, t - 1, :], far[t - 1][:], gb_t[:, t - 1 : t], near[t - 1][:], ALU.mult, ALU.add)
+            if t < PACK:
+                near[t] = near_term(1, t)
+            if t == 0:
+                quantize(z_w[:], z_s[:], z_in[:])
+            if t == 2:
+                quantize(z2_w[0][:], z2_s[0][:], z2_in[0][:])
+                for u in range(PACK):
+                    product(a_bank[u][:, halves[0]], z_w, z_s, u, z2_w[0][:], z2_s[0][:])
+                nc.scalar.activation(pos_win[0][:, halves[0]], a_bank[0][:, halves[0]], ACT.Sigmoid, scale=S_SCALE)
+                nc.scalar.activation(neg_s0[:, halves[0]], a_bank[0][:, halves[0]], ACT.Copy, scale=-S_SCALE)
+                for u in range(1, PACK):
+                    nc.scalar.activation(pos_win[u][:, halves[0]], a_bank[u][:, halves[0]], ACT.Copy, scale=S_SCALE)
+        weave_shared(z2_in[1], z2_rows)
+        quantize(z2_w[1][:], z2_s[1][:], z2_in[1][:])
         for u in range(PACK):
-            product(a_bank[u][:, halves[1]], z_w, z_s, u, z2_w[:], z2_s[:])
+            product(a_bank[u][:, halves[1]], z_w, z_s, u, z2_w[1][:], z2_s[1][:])
 
         gate = [None] + [new("gate%d" % u, [P, N], F32) for u in range(1, PACK)]
         st = [new("st%d" % u, [P, N], F32) for u in range(PACK)]
@@ -268,12 +321,12 @@ def tile_picked_kqminmodlerphopg_none_po_kernel(
         y_in = [new("y_in%d" % h, [P, PACK * HALF], BF16) for h in range(2)]
         y_w = [new("y_w%d" % h, [P, HALF], U32) for h in range(2)]
         y_s = new("y_s", [P, N], U8)
-        weave(nc.scalar.copy, y_in[0], res[0])
+        weave_scalar(y_in[0], res[0], slice(0, HALF))
         hop(2, 1)
         store(1, slice(2, 3))
         hop(3, 1)
         store(1, slice(3, 4))
-        weave(nc.vector.tensor_copy, y_in[1], res[1])
+        weave_shared(y_in[1], res[1])
         words_out = out_1[0].rearrange("p n t -> p (n t)").bitcast(I32)
         for h in range(2):
             nc.vector.quantize_mx(y_w[h][:].bitcast(FP8X4), y_s[:, halves[h]], y_in[h][:])

@@ -15,11 +15,13 @@ ACT = mybir.ActivationFunctionType
 
 P = 128
 PACK = 4
-T = 2048
+QUADRANTS = 4
+TOKENS = 2048
 N = 512
 HALF = N // 2
 LIST_COLS = N // 16
 WIDE = 2 * N
+W2_SCALE_ROW = 4
 S_SCALE = 0.0625
 VECTOR_COLS = 160
 
@@ -34,24 +36,26 @@ def tile_picked_kqminmodlerphopg_none_po_kernel(
     halves = [slice(0, HALF), slice(HALF, N)]
     list_halves = [slice(0, LIST_COLS // 2), slice(LIST_COLS // 2, LIST_COLS)]
 
+    def block(k):
+        return slice(P * k, P * (k + 1))
+
     with ExitStack() as ctx:
         held = ctx.enter_context(tc.tile_pool(name="held", bufs=1))
         ring = ctx.enter_context(tc.tile_pool(name="ring", bufs=2))
         psum = ctx.enter_context(tc.psum_pool(name="psum", bufs=1))
 
-        def new(name, shape, dtype):
-            return held.tile(shape, dtype, name=name, align_bytes=64)
+        def new(name, shape, dtype, tag=None):
+            return held.tile(shape, dtype, name=name, tag=tag or name, align_bytes=64)
 
         def load_list(name, src):
             tile = held.tile([P, LIST_COLS], U16, name=name)
             nc.sync.dma_start(tile[:], src)
             return tile
 
-        def load_scales(queues, tile, first, src):
-            for q in range(4):
-                queues[q].dma_start(
-                    tile[32 * q + first : 32 * q + first + 4, :].bitcast(I32), src[0, 4 * q : 4 * q + 4, :].bitcast(I32)
-                )
+        def load_scales(queues, tile, first_row, src):
+            for q in range(QUADRANTS):
+                rows = slice(32 * q + first_row, 32 * q + first_row + 4)
+                queues[q].dma_start(tile[rows, :].bitcast(I32), src[0, 4 * q : 4 * q + 4, :].bitcast(I32))
 
         def load_words(name, src, width):
             tile = new(name, [P, width], U32)
@@ -65,8 +69,8 @@ def tile_picked_kqminmodlerphopg_none_po_kernel(
             nc.gpsimd.tensor_scalar(negated[:], tile[:], -1.0, 0.0, ALU.mult, ALU.add)
             return tile, negated
 
-        x_sc = new("x_sc", [P, T], U8)
-        w_sc = held.tile([P, N], U8, name="w_sc", tag="w_sc_then_xb_w", align_bytes=64)
+        x_sc = new("x_sc", [P, TOKENS], U8)
+        w_sc = new("w_sc", [P, N], U8, tag="w_sc_then_late_words")
         nc.gpsimd.memset(x_sc[:].bitcast(I32), 0)
         nc.gpsimd.memset(w_sc[:].bitcast(I32), 0)
 
@@ -74,9 +78,9 @@ def tile_picked_kqminmodlerphopg_none_po_kernel(
         l_offs = load_list("l_offs", offs)
         load_scales([nc.sync] * 4, x_sc, 0, x_scales)
         l_two = load_list("l_two", two)
-        x_w = load_words("x_w", x_words, T)
+        x_w = load_words("x_w", x_words, TOKENS)
         load_scales([nc.sync] * 4, w_sc, 0, w1_scales)
-        load_scales([nc.sync] * 3 + [nc.gpsimd], w_sc, 4, w2_scales)
+        load_scales([nc.sync] * 3 + [nc.gpsimd], w_sc, W2_SCALE_ROW, w2_scales)
         ga_t, neg_ga = load_gain("ga_t", ga)
         l_n1 = load_list("l_n1", n1)
         l_n2 = load_list("l_n2", n2)
@@ -97,9 +101,8 @@ def tile_picked_kqminmodlerphopg_none_po_kernel(
         ident = new("ident", [P, P], F32)
         make_identity(nc, ident[:])
 
-        def pick(tile, window, offsets):
-            nc.vector.tensor_copy(tile[:], window[:].indirect(offsets[:]))
-            return tile
+        def pick(dst, window, offsets):
+            nc.vector.tensor_copy(dst, window[:].indirect(offsets))
 
         def deal(name, src, dtype, run):
             dealt = new(name, [P, N], src.dtype)
@@ -109,98 +112,91 @@ def tile_picked_kqminmodlerphopg_none_po_kernel(
             )
             return dealt
 
-        def product(bank, lhs_w, lhs_s, t, rhs_w, rhs_s, first=0):
-            cols = slice(P * t, P * (t + 1))
+        def product(bank, lhs_words, lhs_scales, t, rhs_words, rhs_scales, first_row=0):
             nc.tensor.matmul_mx(
-                out=bank, lhsT=lhs_w[:, cols].bitcast(FP8X4), lhsT_scale=lhs_s[first:, cols],
-                rhs=rhs_w.bitcast(FP8X4), rhs_scale=rhs_s, start=True, stop=True,
+                out=bank, lhsT=lhs_words[:, block(t)].bitcast(FP8X4), lhsT_scale=lhs_scales[first_row:, block(t)],
+                rhs=rhs_words.bitcast(FP8X4), rhs_scale=rhs_scales, start=True, stop=True,
             )
 
+        def quantize(codes, scales, values):
+            nc.vector.quantize_mx(codes.bitcast(FP8X4), scales, values)
+
+        xa_s = new("xa_s", [P, N], U8)
+        xb_s = new("xb_s", [P, N], U8)
+        early_words = new("early_words", [P, HALF], U32)
         w1_dw = deal("w1_dw", w1_w, I32, 4)
-        xa_s = pick(new("xa_s", [P, N], U8), x_sc, l_offs)
-        xb_s = pick(new("xb_s", [P, N], U8), x_sc, l_two)
-        xa_w = pick(new("xa_w", [P, N], U32), x_w, l_offs)
+        pick(xa_s[:], x_sc, l_offs[:])
+        pick(xb_s[:], x_sc, l_two[:])
+        pick(early_words[:], x_w, l_offs[:, list_halves[0]])
         w_ds = deal("w_ds", w_sc, U8, 16)
-        xb_w = pick(held.tile([P, N], U32, name="xb_w", tag="w_sc_then_xb_w", align_bytes=64), x_w, l_two)
+        late_words = new("late_words", [P, HALF + N], U32, tag="w_sc_then_late_words")
+        xa_w = [early_words[:], late_words[:, :HALF]]
+        xb_w = late_words[:, HALF:]
+        pick(xa_w[1], x_w, l_offs[:, list_halves[1]])
+        pick(xb_w, x_w, l_two[:])
         w2_dw = deal("w2_dw", w2_w, I32, 4)
 
         a_bank = [psum.tile([P, N], F32, name="a_bank%d" % t) for t in range(PACK)]
         b_bank = [psum.tile([P, N], F32, name="b_bank%d" % t) for t in range(PACK)]
-        for t in range(PACK):
-            product(a_bank[t][:], w1_dw, w_ds, t, xa_w[:], xa_s[:])
-        for t in range(PACK):
-            product(b_bank[t][:], w2_dw, w_ds, t, xb_w[:], xb_s[:], first=4)
 
+        def a_copies(t, cols, bank):
+            nc.scalar.activation(neg_win[t][:, cols], bank, ACT.Copy, scale=neg_ga[:, t : t + 1])
+            nc.scalar.activation(pos_win[t][:, cols], bank, ACT.Copy, scale=ga_t[:, t : t + 1])
 
+        for h, bank in enumerate((a_bank[0], b_bank[PACK - 1])):
+            product(bank[:, :HALF], w1_dw, w_ds, 0, xa_w[h], xa_s[:, halves[h]])
+            a_copies(0, halves[h], bank[:, :HALF])
+        for t in range(1, PACK):
+            for h in range(2):
+                product(a_bank[t][:, halves[h]], w1_dw, w_ds, t, xa_w[h], xa_s[:, halves[h]])
+            a_copies(t, slice(0, N), a_bank[t][:])
         for t in range(PACK):
-            nc.scalar.activation(pos_win[t][:, :N], a_bank[t][:], ACT.Copy, scale=ga_t[:, t : t + 1])
-            nc.scalar.activation(neg_win[t][:, :N], a_bank[t][:], ACT.Copy, scale=neg_ga[:, t : t + 1])
+            product(b_bank[t][:], w2_dw, w_ds, t, xb_w, xb_s[:], first_row=W2_SCALE_ROW)
+
         b_win = [new("b_win%d" % t, [P, N], F32) for t in range(PACK)]
-        sig = [[new("sig%d%d" % (h, t), [P, HALF], F32) for t in range(PACK)] for h in range(2)]
-        rest = [[new("rest%d%d" % (h, t), [P, HALF], F32) for t in range(PACK)] for h in range(2)]
+        far_weight = [[new("far_weight%d%d" % (h, t), [P, HALF], F32) for t in range(PACK)] for h in range(2)]
+        near_weight = [[new("near_weight%d%d" % (h, t), [P, HALF], F32) for t in range(PACK)] for h in range(2)]
 
         def b_copy(t):
             nc.scalar.copy(b_win[t][:], b_bank[t][:])
 
         def mix_weights(h, t):
-            nc.scalar.activation(sig[h][t][:], b_win[t][:].indirect(l_n4[:, list_halves[h]]), ACT.Sigmoid)
-            nc.scalar.activation(
-                rest[h][t][:], sig[h][t][:], ACT.Identity,
-                scale=neg_gb[:, t : t + 1], bias=gb_t[:, t : t + 1],
-            )
+            far, near, gain = far_weight[h][t][:], near_weight[h][t][:], gb_t[:, t : t + 1]
+            nc.scalar.activation(far, b_win[t][:].indirect(l_n4[:, list_halves[h]]), ACT.Sigmoid)
+            nc.scalar.activation(near, far, ACT.Identity, scale=neg_gb[:, t : t + 1], bias=gain)
             if h == 0:
-                nc.scalar.activation(sig[h][t][:], sig[h][t][:], ACT.Copy, scale=gb_t[:, t : t + 1])
+                nc.scalar.activation(far, far, ACT.Copy, scale=gain)
 
-        between = [
-            [lambda: b_copy(0)],
-            [lambda: b_copy(1), lambda: b_copy(2), lambda: b_copy(3), lambda: mix_weights(0, 0)],
-            [lambda: mix_weights(0, 1), lambda: mix_weights(0, 2), lambda: mix_weights(0, 3)],
-            [lambda: mix_weights(1, 0), lambda: mix_weights(1, 1), lambda: mix_weights(1, 2), lambda: mix_weights(1, 3)],
-        ]
+        preparation = [(b_copy, (t,)) for t in range(PACK)]
+        preparation.extend((mix_weights, (h, t)) for h in range(2) for t in range(PACK))
+        cuts = (0, 1, 5, 8, 12)
 
         z_rows = new("z_rows", [P, PACK, N], BF16)
-        pa, pb, low, high = {}, {}, {}, {}
+        pa, pb, floor, cap = {}, {}, {}, {}
         for t in range(PACK + 1):
             if t < PACK:
                 pa[t] = ring.tile([P, N], F32, name="pa")
                 nc.vector.tensor_tensor(pa[t][:], neg_win[t][:].indirect(l_n1[:]), pos_win[t][:, :N], ALU.add)
-                high[t] = ring.tile([P, N], BF16, name="high")
-                nc.scalar.activation(high[t][:], pa[t][:], ACT.Relu)
-                for step in between[t]:
-                    step()
+                cap[t] = ring.tile([P, N], BF16, name="cap")
+                nc.scalar.activation(cap[t][:], pa[t][:], ACT.Relu)
+                for step, arguments in preparation[cuts[t] : cuts[t + 1]]:
+                    step(*arguments)
             if t > 0:
-                low[t - 1] = ring.tile([P, N], BF16, name="low")
-                nc.vector.scalar_tensor_tensor(low[t - 1][:], pa[t - 1][:], 0.0, pb[t - 1][:], ALU.min, ALU.max)
+                floor[t - 1] = ring.tile([P, N], BF16, name="floor")
+                nc.vector.scalar_tensor_tensor(floor[t - 1][:], pa[t - 1][:], 0.0, pb[t - 1][:], ALU.min, ALU.max)
             if t < PACK:
                 pb[t] = ring.tile([P, N], F32, name="pb")
                 nc.vector.tensor_tensor(pb[t][:], pos_win[t][:].indirect(l_n2[:]), neg_win[t][:, :N], ALU.add)
             if t > 0:
-                nc.vector.tensor_tensor(z_rows[:, t - 1, :], high[t - 1][:], low[t - 1][:], ALU.min)
+                nc.vector.tensor_tensor(z_rows[:, t - 1, :], cap[t - 1][:], floor[t - 1][:], ALU.min)
 
         z_in = new("z_in", [P, PACK * N], BF16)
-        nc.scalar.copy(
-            z_in[:].rearrange("p (u c i t) -> p c t i u", u=PACK, i=2, t=PACK),
-            z_rows[:].rearrange("p t (c i u) -> p c t i u", i=2, u=PACK),
-        )
         z_w = new("z_w", [P, N], U32)
         z_s = new("z_s", [P, N], U8)
 
-        def weave_scalar(dst, src, cols):
-            nc.scalar.copy(
-                dst[:].rearrange("p (c t) -> p c t", t=PACK)[:, cols, :].rearrange("p (c i) t -> p c t i", i=4),
-                src[:, :, cols].rearrange("p t (c i) -> p c t i", i=4),
-            )
-
-        def weave_shared(dst, src):
-            cols = slice(0, VECTOR_COLS)
-            nc.vector.tensor_copy(
-                dst[:].rearrange("p (c t) -> p c t", t=PACK)[:, cols, :], src[:, :, cols].rearrange("p t c -> p c t")
-            )
-            weave_scalar(dst, src, slice(VECTOR_COLS, HALF))
-
         neg_s0 = new("neg_s0", [P, N], F32)
         z2_in = [
-            held.tile([P, PACK * HALF], BF16, name="z2_in0", tag="z2_in0_then_far", align_bytes=64),
+            new("z2_in0", [P, PACK * HALF], BF16, tag="z2_in0_then_last_far"),
             new("z2_in1", [P, PACK * HALF], BF16),
         ]
         z2_w = [new("z2_w%d" % h, [P, HALF], U32) for h in range(2)]
@@ -208,41 +204,52 @@ def tile_picked_kqminmodlerphopg_none_po_kernel(
 
         def far_term(h, t):
             if (h, t) == (1, PACK - 1):
-                far = held.tile([P, HALF], F32, name="last_far", tag="z2_in0_then_far", align_bytes=64)
+                far = new("last_far", [P, HALF], F32, tag="z2_in0_then_last_far")
             else:
                 far = ring.tile([P, HALF], F32, name="far")
-            nc.vector.tensor_tensor(far[:], b_win[t][:].indirect(l_n5[:, list_halves[h]]), sig[h][t][:], ALU.mult)
+            nc.vector.tensor_tensor(
+                far[:], b_win[t][:].indirect(l_n5[:, list_halves[h]]), far_weight[h][t][:], ALU.mult
+            )
             return far
 
         def near_term(h, t):
             near = ring.tile([P, HALF], F32, name="near")
-            nc.vector.tensor_tensor(near[:], b_win[t][:].indirect(l_n3[:, list_halves[h]]), rest[h][t][:], ALU.mult)
+            nc.vector.tensor_tensor(
+                near[:], b_win[t][:].indirect(l_n3[:, list_halves[h]]), near_weight[h][t][:], ALU.mult
+            )
             return near
-
-        def quantize(codes, scales, values):
-            nc.vector.quantize_mx(codes.bitcast(FP8X4), scales, values)
-
-        def block(k):
-            return slice(P * k, P * (k + 1))
 
         sum_bank, word_bank = b_bank[:2], b_bank[2]
         for t in range(PACK):
-            far, near = far_term(0, t), near_term(0, t)
+            terms = (far_term(0, t), near_term(0, t))
             for k in range(2):
-                nc.tensor.matmul(sum_bank[k][:, block(t)], far[:, block(k)], ident[:], start=True, stop=False, is_transpose=True)
-                nc.tensor.matmul(sum_bank[k][:, block(t)], near[:, block(k)], ident[:], start=False, stop=True, is_transpose=True)
+                for place, term in enumerate(terms):
+                    nc.tensor.matmul(
+                        sum_bank[k][:, block(t)], term[:, block(k)], ident[:],
+                        start=place == 0, stop=place == 1, is_transpose=True,
+                    )
         for k in range(2):
             turned = new("turned%d" % k, [P, N], BF16)
             nc.scalar.copy(
-                turned[:].rearrange("v (u p s) -> v u p s", u=2, s=2),
-                sum_bank[k][:].rearrange("v (u s p) -> v u p s", u=2, s=2),
+                turned[:].rearrange("v (u p e) -> v u p e", u=2, e=2),
+                sum_bank[k][:].rearrange("v (u e p) -> v u p e", u=2, e=2),
             )
             for u in range(2):
                 nc.tensor.transpose(word_bank[:, block(2 * k + u)], turned[:].bitcast(F32)[:, block(u)], ident[:])
         nc.scalar.copy(
+            z_in[:].rearrange("p (r c i t) -> p c t i r", r=PACK, i=2, t=PACK),
+            z_rows[:].rearrange("p t (c i r) -> p c t i r", i=2, r=PACK),
+        )
+        nc.scalar.copy(
             z2_in[0][:].bitcast(F32).rearrange("p (k v u) -> p k v u", k=2, u=2),
             word_bank[:].rearrange("p (k u v) -> p k v u", k=2, u=2),
         )
+
+        def s_copy(r, h):
+            nc.scalar.activation(pos_win[r][:, halves[h]], a_bank[r][:, halves[h]], ACT.Copy, scale=S_SCALE)
+
+        def s_sigmoid(h):
+            nc.scalar.activation(pos_win[0][:, halves[h]], a_bank[0][:, halves[h]], ACT.Sigmoid, scale=S_SCALE)
 
         z2_rows = new("z2_rows", [P, PACK, HALF], BF16)
         far, near = {}, {}
@@ -251,88 +258,86 @@ def tile_picked_kqminmodlerphopg_none_po_kernel(
                 far[t] = far_term(1, t)
             if t > 0:
                 nc.vector.scalar_tensor_tensor(
-                    z2_rows[:, t - 1, :], far[t - 1][:], gb_t[:, t - 1 : t], near[t - 1][:], ALU.mult, ALU.add)
+                    z2_rows[:, t - 1, :], far[t - 1][:], gb_t[:, t - 1 : t], near[t - 1][:], ALU.mult, ALU.add
+                )
             if t < PACK:
                 near[t] = near_term(1, t)
             if t == 0:
                 quantize(z_w[:], z_s[:], z_in[:])
-            if t == 2:
+            if t == PACK - 2:
                 quantize(z2_w[0][:], z2_s[0][:], z2_in[0][:])
-                for u in range(PACK):
-                    product(a_bank[u][:, halves[0]], z_w, z_s, u, z2_w[0][:], z2_s[0][:])
-                nc.scalar.activation(pos_win[0][:, halves[0]], a_bank[0][:, halves[0]], ACT.Sigmoid, scale=S_SCALE)
+                for r in range(PACK):
+                    product(a_bank[r][:, halves[0]], z_w, z_s, r, z2_w[0][:], z2_s[0][:])
+                s_sigmoid(0)
                 nc.scalar.activation(neg_s0[:, halves[0]], a_bank[0][:, halves[0]], ACT.Copy, scale=-S_SCALE)
-                for u in range(1, PACK):
-                    nc.scalar.activation(pos_win[u][:, halves[0]], a_bank[u][:, halves[0]], ACT.Copy, scale=S_SCALE)
-        weave_shared(z2_in[1], z2_rows)
+                for r in range(1, PACK):
+                    s_copy(r, 0)
+        nc.vector.tensor_copy(
+            z2_in[1][:].rearrange("p (c t) -> p c t", t=PACK), z2_rows[:].rearrange("p t c -> p c t")
+        )
         quantize(z2_w[1][:], z2_s[1][:], z2_in[1][:])
-        for u in range(PACK):
-            product(a_bank[u][:, halves[1]], z_w, z_s, u, z2_w[1][:], z2_s[1][:])
+        for r in range(PACK):
+            product(a_bank[r][:, halves[1]], z_w, z_s, r, z2_w[1][:], z2_s[1][:])
 
-        gate = [None] + [new("gate%d" % u, [P, N], F32) for u in range(1, PACK)]
-        st = [new("st%d" % u, [P, N], F32) for u in range(PACK)]
-        res = [new("res%d" % h, [P, PACK, HALF], F32) for h in range(2)]
-        out_rows = out_0.rearrange("(p u) v -> p u v", u=PACK)
+        gate = {r: new("gate%d" % r, [P, N], F32) for r in range(1, PACK)}
+        st = [new("st%d" % r, [P, N], F32) for r in range(PACK)]
+        res = new("res", [P, PACK, N], F32)
+        out_rows = out_0.rearrange("(p r) v -> p r v", r=PACK)
 
-        def s_copy(u):
-            nc.scalar.activation(pos_win[u][:, halves[1]], a_bank[u][:, halves[1]], ACT.Copy, scale=S_SCALE)
+        def gate_gather(r):
+            nc.scalar.activation(gate[r][:], pos_win[r][:].indirect(l_n6[:]), ACT.Sigmoid)
 
-        def gate_gather(u):
-            nc.scalar.activation(gate[u][:], pos_win[u][:].indirect(l_n6[:]), ACT.Sigmoid)
+        def flip(r):
+            nc.scalar.activation(st[r][:], neg_win[r][:, :N], ACT.Copy, scale=-1.0)
 
-        def neg_st(u):
-            nc.vector.scalar_tensor_tensor(neg_win[u][:, :N], a_bank[u][:], -S_SCALE, gate[u][:], ALU.mult, ALU.mult)
-
-        def flip(u):
-            nc.scalar.activation(st[u][:], neg_win[u][:, :N], ACT.Copy, scale=-1.0)
-
-        def hop(u, h):
+        def hop(r, cols, list_cols):
             nc.vector.tensor_tensor(
-                res[h][:, u, :], neg_win[u][:].indirect(l_n7[:, list_halves[h]]), st[u][:, halves[h]], ALU.add)
+                res[:, r, cols], neg_win[r][:].indirect(l_n7[:, list_cols]), st[r][:, cols], ALU.add
+            )
+            nc.sync.dma_start(out_rows[:, r, cols], res[:, r, cols])
 
-        def store(h, us):
-            nc.sync.dma_start(out_rows[:, us, halves[h]], res[h][:, us, :])
-
-        nc.scalar.activation(pos_win[0][:, halves[1]], a_bank[0][:, halves[1]], ACT.Sigmoid, scale=S_SCALE)
+        s_sigmoid(1)
         nc.vector.tensor_scalar(pos_win[1][:, halves[1]], a_bank[1][:, halves[1]], S_SCALE, None, ALU.mult)
         nc.vector.tensor_scalar(neg_s0[:, halves[1]], a_bank[0][:, halves[1]], -S_SCALE, None, ALU.mult)
         gate_gather(1)
         nc.vector.tensor_tensor(neg_win[0][:, :N], pos_win[0][:].indirect(l_n6[:]), neg_s0[:], ALU.mult)
-        s_copy(2)
-        flip(0)
-        neg_st(1)
-        gate_gather(2)
-        hop(0, 0)
-        hop(0, 1)
-        flip(1)
-        s_copy(3)
-        neg_st(2)
-        gate_gather(3)
-        hop(1, 0)
-        hop(1, 1)
-        store(0, slice(0, 2))
-        store(1, slice(0, 2))
-        flip(2)
-        neg_st(3)
-        flip(3)
-        hop(2, 0)
-        hop(3, 0)
-        store(0, slice(2, 4))
+        for r in range(1, PACK):
+            flip(r - 1)
+            if r + 1 < PACK:
+                s_copy(r + 1, 1)
+            nc.vector.scalar_tensor_tensor(neg_win[r][:, :N], a_bank[r][:], -S_SCALE, gate[r][:], ALU.mult, ALU.mult)
+            if r + 1 < PACK:
+                gate_gather(r + 1)
+                hop(r - 1, slice(0, N), slice(0, LIST_COLS))
+        flip(PACK - 1)
+
         y_in = [new("y_in%d" % h, [P, PACK * HALF], BF16) for h in range(2)]
         y_w = [new("y_w%d" % h, [P, HALF], U32) for h in range(2)]
         y_s = new("y_s", [P, N], U8)
-        weave_scalar(y_in[0], res[0], slice(0, HALF))
-        hop(2, 1)
-        store(1, slice(2, 3))
-        hop(3, 1)
-        store(1, slice(3, 4))
-        weave_shared(y_in[1], res[1])
+
+        def woven(h, cols):
+            return y_in[h][:].rearrange("p (c r) -> p c r", r=PACK)[:, cols, :]
+
+        def weave_on_scalar(h, cols):
+            nc.scalar.copy(
+                woven(h, cols).rearrange("p (c i) r -> p c r i", i=4),
+                res[:, :, halves[h]][:, :, cols].rearrange("p r (c i) -> p c r i", i=4),
+            )
+
+        for h in range(2):
+            for r in range(PACK - 2, PACK):
+                hop(r, halves[h], list_halves[h])
+            if h == 0:
+                weave_on_scalar(0, slice(0, HALF))
+        nc.vector.tensor_copy(
+            woven(1, slice(0, VECTOR_COLS)), res[:, :, HALF : HALF + VECTOR_COLS].rearrange("p r c -> p c r")
+        )
+        weave_on_scalar(1, slice(VECTOR_COLS, HALF))
+
         words_out = out_1[0].rearrange("p n t -> p (n t)").bitcast(I32)
         for h in range(2):
-            nc.vector.quantize_mx(y_w[h][:].bitcast(FP8X4), y_s[:, halves[h]], y_in[h][:])
+            quantize(y_w[h][:], y_s[:, halves[h]], y_in[h][:])
             nc.sync.dma_start(words_out[:, halves[h]], y_w[h][:].bitcast(I32))
-        for q in range(4):
+        for q in range(QUADRANTS):
             queue = nc.scalar if q % 2 else nc.sync
-            queue.dma_start(
-                out_2[0, 4 * q : 4 * q + 4, :].bitcast(I32), y_s[32 * q : 32 * q + 4, :].bitcast(I32)
-            )
+            queue.dma_start(out_2[0, 4 * q : 4 * q + 4, :].bitcast(I32), y_s[32 * q : 32 * q + 4, :].bitcast(I32))

from contextlib import ExitStack

import concourse.mybir as mybir
from concourse.masks import make_identity

F32 = mybir.dt.float32
BF16 = mybir.dt.bfloat16
I32 = mybir.dt.int32
U32 = mybir.dt.uint32
U16 = mybir.dt.uint16
U8 = mybir.dt.uint8
FP8X4 = mybir.dt.float8_e4m3fn_x4
ALU = mybir.AluOpType
ACT = mybir.ActivationFunctionType

P = 128
PACK = 4
QUADRANTS = 4
TOKENS = 2048
N = 512
HALF = N // 2
LIST_COLS = N // 16
WIDE = 2 * N
W2_SCALE_ROW = 4
S_SCALE = 0.0625
VECTOR_COLS = 160

FLOPS = 3 * 2 * 512 * 512 * 512


def tile_picked_kqminmodlerphopg_none_po_kernel(
    tc, x_words, x_scales, w1_words, w1_scales, w2_words, w2_scales, ga, gb,
    offs, two, n1, n2, n3, n4, n5, n6, n7, out_0, out_1, out_2,
):
    nc = tc.nc
    halves = [slice(0, HALF), slice(HALF, N)]
    list_halves = [slice(0, LIST_COLS // 2), slice(LIST_COLS // 2, LIST_COLS)]

    def block(k):
        return slice(P * k, P * (k + 1))

    with ExitStack() as ctx:
        held = ctx.enter_context(tc.tile_pool(name="held", bufs=1))
        ring = ctx.enter_context(tc.tile_pool(name="ring", bufs=2))
        psum = ctx.enter_context(tc.psum_pool(name="psum", bufs=1))

        def new(name, shape, dtype, tag=None):
            return held.tile(shape, dtype, name=name, tag=tag or name, align_bytes=64)

        def load_list(name, src):
            tile = held.tile([P, LIST_COLS], U16, name=name)
            nc.sync.dma_start(tile[:], src)
            return tile

        def load_scales(queues, tile, first_row, src):
            for q in range(QUADRANTS):
                rows = slice(32 * q + first_row, 32 * q + first_row + 4)
                queues[q].dma_start(tile[rows, :].bitcast(I32), src[0, 4 * q : 4 * q + 4, :].bitcast(I32))

        def load_words(name, src, width):
            tile = new(name, [P, width], U32)
            nc.sync.dma_start(tile[:].bitcast(I32), src[0].rearrange("p n t -> p (n t)").bitcast(I32))
            return tile

        def load_gain(name, src):
            tile = new(name, [P, PACK], F32)
            negated = new("neg_" + name, [P, PACK], F32)
            nc.gpsimd.dma_start(tile[:], src.rearrange("(p t) o -> p (t o)", t=PACK))
            nc.gpsimd.tensor_scalar(negated[:], tile[:], -1.0, 0.0, ALU.mult, ALU.add)
            return tile, negated

        x_sc = new("x_sc", [P, TOKENS], U8)
        w_sc = new("w_sc", [P, N], U8, tag="w_sc_then_late_words")
        nc.gpsimd.memset(x_sc[:].bitcast(I32), 0)
        nc.gpsimd.memset(w_sc[:].bitcast(I32), 0)

        w1_w = load_words("w1_w", w1_words, N)
        l_offs = load_list("l_offs", offs)
        load_scales([nc.sync] * 4, x_sc, 0, x_scales)
        l_two = load_list("l_two", two)
        x_w = load_words("x_w", x_words, TOKENS)
        load_scales([nc.sync] * 4, w_sc, 0, w1_scales)
        load_scales([nc.sync] * 3 + [nc.gpsimd], w_sc, W2_SCALE_ROW, w2_scales)
        ga_t, neg_ga = load_gain("ga_t", ga)
        l_n1 = load_list("l_n1", n1)
        l_n2 = load_list("l_n2", n2)
        w2_w = load_words("w2_w", w2_words, N)
        gb_t, neg_gb = load_gain("gb_t", gb)
        l_n4 = load_list("l_n4", n4)
        l_n5 = load_list("l_n5", n5)
        l_n3 = load_list("l_n3", n3)
        l_n6 = load_list("l_n6", n6)
        l_n7 = load_list("l_n7", n7)

        pos_win = [new("pos_win%d" % t, [P, WIDE], F32) for t in range(PACK)]
        neg_win = [new("neg_win%d" % t, [P, WIDE], F32) for t in range(PACK)]
        for t in range(PACK):
            nc.vector.memset(pos_win[t][:, N:], 0.0)
            nc.scalar.activation(neg_win[t][:, N:], pos_win[t][:, N:], ACT.Sigmoid)

        ident = new("ident", [P, P], F32)
        make_identity(nc, ident[:])

        def pick(dst, window, offsets):
            nc.vector.tensor_copy(dst, window[:].indirect(offsets))

        def deal(name, src, dtype, run):
            dealt = new(name, [P, N], src.dtype)
            nc.vector.tensor_copy(
                dealt[:].bitcast(dtype).rearrange("p (t c i) -> p c t i", t=PACK, i=run),
                src[:].bitcast(dtype).rearrange("p (c i t) -> p c t i", t=PACK, i=run),
            )
            return dealt

        def product(bank, lhs_words, lhs_scales, t, rhs_words, rhs_scales, first_row=0):
            nc.tensor.matmul_mx(
                out=bank, lhsT=lhs_words[:, block(t)].bitcast(FP8X4), lhsT_scale=lhs_scales[first_row:, block(t)],
                rhs=rhs_words.bitcast(FP8X4), rhs_scale=rhs_scales, start=True, stop=True,
            )

        def quantize(codes, scales, values):
            nc.vector.quantize_mx(codes.bitcast(FP8X4), scales, values)

        xa_s = new("xa_s", [P, N], U8)
        xb_s = new("xb_s", [P, N], U8)
        early_words = new("early_words", [P, HALF], U32)
        w1_dw = deal("w1_dw", w1_w, I32, 4)
        pick(xa_s[:], x_sc, l_offs[:])
        pick(xb_s[:], x_sc, l_two[:])
        pick(early_words[:], x_w, l_offs[:, list_halves[0]])
        w_ds = deal("w_ds", w_sc, U8, 16)
        late_words = new("late_words", [P, HALF + N], U32, tag="w_sc_then_late_words")
        xa_w = [early_words[:], late_words[:, :HALF]]
        xb_w = late_words[:, HALF:]
        pick(xa_w[1], x_w, l_offs[:, list_halves[1]])
        pick(xb_w, x_w, l_two[:])
        w2_dw = deal("w2_dw", w2_w, I32, 4)

        a_bank = [psum.tile([P, N], F32, name="a_bank%d" % t) for t in range(PACK)]
        b_bank = [psum.tile([P, N], F32, name="b_bank%d" % t) for t in range(PACK)]

        def a_copies(t, cols, bank):
            nc.scalar.activation(neg_win[t][:, cols], bank, ACT.Copy, scale=neg_ga[:, t : t + 1])
            nc.scalar.activation(pos_win[t][:, cols], bank, ACT.Copy, scale=ga_t[:, t : t + 1])

        for h, bank in enumerate((a_bank[0], b_bank[PACK - 1])):
            product(bank[:, :HALF], w1_dw, w_ds, 0, xa_w[h], xa_s[:, halves[h]])
            a_copies(0, halves[h], bank[:, :HALF])
        for t in range(1, PACK):
            for h in range(2):
                product(a_bank[t][:, halves[h]], w1_dw, w_ds, t, xa_w[h], xa_s[:, halves[h]])
            a_copies(t, slice(0, N), a_bank[t][:])
        for t in range(PACK):
            product(b_bank[t][:], w2_dw, w_ds, t, xb_w, xb_s[:], first_row=W2_SCALE_ROW)

        b_win = [new("b_win%d" % t, [P, N], F32) for t in range(PACK)]
        far_weight = [[new("far_weight%d%d" % (h, t), [P, HALF], F32) for t in range(PACK)] for h in range(2)]
        near_weight = [[new("near_weight%d%d" % (h, t), [P, HALF], F32) for t in range(PACK)] for h in range(2)]

        def b_copy(t):
            nc.scalar.copy(b_win[t][:], b_bank[t][:])

        def mix_weights(h, t):
            far, near, gain = far_weight[h][t][:], near_weight[h][t][:], gb_t[:, t : t + 1]
            nc.scalar.activation(far, b_win[t][:].indirect(l_n4[:, list_halves[h]]), ACT.Sigmoid)
            nc.scalar.activation(near, far, ACT.Identity, scale=neg_gb[:, t : t + 1], bias=gain)
            if h == 0:
                nc.scalar.activation(far, far, ACT.Copy, scale=gain)

        preparation = [(b_copy, (t,)) for t in range(PACK)]
        preparation.extend((mix_weights, (h, t)) for h in range(2) for t in range(PACK))
        cuts = (0, 1, 5, 8, 12)

        z_rows = new("z_rows", [P, PACK, N], BF16)
        pa, pb, floor, cap = {}, {}, {}, {}
        for t in range(PACK + 1):
            if t < PACK:
                pa[t] = ring.tile([P, N], F32, name="pa")
                nc.vector.tensor_tensor(pa[t][:], neg_win[t][:].indirect(l_n1[:]), pos_win[t][:, :N], ALU.add)
                cap[t] = ring.tile([P, N], BF16, name="cap")
                nc.scalar.activation(cap[t][:], pa[t][:], ACT.Relu)
                for step, arguments in preparation[cuts[t] : cuts[t + 1]]:
                    step(*arguments)
            if t > 0:
                floor[t - 1] = ring.tile([P, N], BF16, name="floor")
                nc.vector.scalar_tensor_tensor(floor[t - 1][:], pa[t - 1][:], 0.0, pb[t - 1][:], ALU.min, ALU.max)
            if t < PACK:
                pb[t] = ring.tile([P, N], F32, name="pb")
                nc.vector.tensor_tensor(pb[t][:], pos_win[t][:].indirect(l_n2[:]), neg_win[t][:, :N], ALU.add)
            if t > 0:
                nc.vector.tensor_tensor(z_rows[:, t - 1, :], cap[t - 1][:], floor[t - 1][:], ALU.min)

        z_in = new("z_in", [P, PACK * N], BF16)
        z_w = new("z_w", [P, N], U32)
        z_s = new("z_s", [P, N], U8)

        neg_s0 = new("neg_s0", [P, N], F32)
        z2_in = [
            new("z2_in0", [P, PACK * HALF], BF16, tag="z2_in0_then_last_far"),
            new("z2_in1", [P, PACK * HALF], BF16),
        ]
        z2_w = [new("z2_w%d" % h, [P, HALF], U32) for h in range(2)]
        z2_s = [new("z2_s%d" % h, [P, HALF], U8) for h in range(2)]

        def far_term(h, t):
            if (h, t) == (1, PACK - 1):
                far = new("last_far", [P, HALF], F32, tag="z2_in0_then_last_far")
            else:
                far = ring.tile([P, HALF], F32, name="far")
            nc.vector.tensor_tensor(
                far[:], b_win[t][:].indirect(l_n5[:, list_halves[h]]), far_weight[h][t][:], ALU.mult
            )
            return far

        def near_term(h, t):
            near = ring.tile([P, HALF], F32, name="near")
            nc.vector.tensor_tensor(
                near[:], b_win[t][:].indirect(l_n3[:, list_halves[h]]), near_weight[h][t][:], ALU.mult
            )
            return near

        sum_bank, word_bank = b_bank[:2], b_bank[2]
        for t in range(PACK):
            terms = (far_term(0, t), near_term(0, t))
            for k in range(2):
                for place, term in enumerate(terms):
                    nc.tensor.matmul(
                        sum_bank[k][:, block(t)], term[:, block(k)], ident[:],
                        start=place == 0, stop=place == 1, is_transpose=True,
                    )
        for k in range(2):
            turned = new("turned%d" % k, [P, N], BF16)
            nc.scalar.copy(
                turned[:].rearrange("v (u p e) -> v u p e", u=2, e=2),
                sum_bank[k][:].rearrange("v (u e p) -> v u p e", u=2, e=2),
            )
            for u in range(2):
                nc.tensor.transpose(word_bank[:, block(2 * k + u)], turned[:].bitcast(F32)[:, block(u)], ident[:])
        nc.scalar.copy(
            z_in[:].rearrange("p (r c i t) -> p c t i r", r=PACK, i=2, t=PACK),
            z_rows[:].rearrange("p t (c i r) -> p c t i r", i=2, r=PACK),
        )
        nc.scalar.copy(
            z2_in[0][:].bitcast(F32).rearrange("p (k v u) -> p k v u", k=2, u=2),
            word_bank[:].rearrange("p (k u v) -> p k v u", k=2, u=2),
        )

        def s_copy(r, h):
            nc.scalar.activation(pos_win[r][:, halves[h]], a_bank[r][:, halves[h]], ACT.Copy, scale=S_SCALE)

        def s_sigmoid(h):
            nc.scalar.activation(pos_win[0][:, halves[h]], a_bank[0][:, halves[h]], ACT.Sigmoid, scale=S_SCALE)

        z2_rows = new("z2_rows", [P, PACK, HALF], BF16)
        far, near = {}, {}
        for t in range(PACK + 1):
            if t < PACK:
                far[t] = far_term(1, t)
            if t > 0:
                nc.vector.scalar_tensor_tensor(
                    z2_rows[:, t - 1, :], far[t - 1][:], gb_t[:, t - 1 : t], near[t - 1][:], ALU.mult, ALU.add
                )
            if t < PACK:
                near[t] = near_term(1, t)
            if t == 0:
                quantize(z_w[:], z_s[:], z_in[:])
            if t == PACK - 2:
                quantize(z2_w[0][:], z2_s[0][:], z2_in[0][:])
                for r in range(PACK):
                    product(a_bank[r][:, halves[0]], z_w, z_s, r, z2_w[0][:], z2_s[0][:])
                s_sigmoid(0)
                nc.scalar.activation(neg_s0[:, halves[0]], a_bank[0][:, halves[0]], ACT.Copy, scale=-S_SCALE)
                for r in range(1, PACK):
                    s_copy(r, 0)
        nc.vector.tensor_copy(
            z2_in[1][:].rearrange("p (c t) -> p c t", t=PACK), z2_rows[:].rearrange("p t c -> p c t")
        )
        quantize(z2_w[1][:], z2_s[1][:], z2_in[1][:])
        for r in range(PACK):
            product(a_bank[r][:, halves[1]], z_w, z_s, r, z2_w[1][:], z2_s[1][:])

        gate = {r: new("gate%d" % r, [P, N], F32) for r in range(1, PACK)}
        st = [new("st%d" % r, [P, N], F32) for r in range(PACK)]
        res = new("res", [P, PACK, N], F32)
        out_rows = out_0.rearrange("(p r) v -> p r v", r=PACK)

        def gate_gather(r):
            nc.scalar.activation(gate[r][:], pos_win[r][:].indirect(l_n6[:]), ACT.Sigmoid)

        def flip(r):
            nc.scalar.activation(st[r][:], neg_win[r][:, :N], ACT.Copy, scale=-1.0)

        def hop(r, cols, list_cols):
            nc.vector.tensor_tensor(
                res[:, r, cols], neg_win[r][:].indirect(l_n7[:, list_cols]), st[r][:, cols], ALU.add
            )
            nc.sync.dma_start(out_rows[:, r, cols], res[:, r, cols])

        s_sigmoid(1)
        nc.vector.tensor_scalar(pos_win[1][:, halves[1]], a_bank[1][:, halves[1]], S_SCALE, None, ALU.mult)
        nc.vector.tensor_scalar(neg_s0[:, halves[1]], a_bank[0][:, halves[1]], -S_SCALE, None, ALU.mult)
        gate_gather(1)
        nc.vector.tensor_tensor(neg_win[0][:, :N], pos_win[0][:].indirect(l_n6[:]), neg_s0[:], ALU.mult)
        for r in range(1, PACK):
            flip(r - 1)
            if r + 1 < PACK:
                s_copy(r + 1, 1)
            nc.vector.scalar_tensor_tensor(neg_win[r][:, :N], a_bank[r][:], -S_SCALE, gate[r][:], ALU.mult, ALU.mult)
            if r + 1 < PACK:
                gate_gather(r + 1)
                hop(r - 1, slice(0, N), slice(0, LIST_COLS))
        flip(PACK - 1)

        y_in = [new("y_in%d" % h, [P, PACK * HALF], BF16) for h in range(2)]
        y_w = [new("y_w%d" % h, [P, HALF], U32) for h in range(2)]
        y_s = new("y_s", [P, N], U8)

        def woven(h, cols):
            return y_in[h][:].rearrange("p (c r) -> p c r", r=PACK)[:, cols, :]

        def weave_on_scalar(h, cols):
            nc.scalar.copy(
                woven(h, cols).rearrange("p (c i) r -> p c r i", i=4),
                res[:, :, halves[h]][:, :, cols].rearrange("p r (c i) -> p c r i", i=4),
            )

        for h in range(2):
            for r in range(PACK - 2, PACK):
                hop(r, halves[h], list_halves[h])
            if h == 0:
                weave_on_scalar(0, slice(0, HALF))
        nc.vector.tensor_copy(
            woven(1, slice(0, VECTOR_COLS)), res[:, :, HALF : HALF + VECTOR_COLS].rearrange("p r c -> p c r")
        )
        weave_on_scalar(1, slice(VECTOR_COLS, HALF))

        words_out = out_1[0].rearrange("p n t -> p (n t)").bitcast(I32)
        for h in range(2):
            quantize(y_w[h][:], y_s[:, halves[h]], y_in[h][:])
            nc.sync.dma_start(words_out[:, halves[h]], y_w[h][:].bitcast(I32))
        for q in range(QUADRANTS):
            queue = nc.scalar if q % 2 else nc.sync
            queue.dma_start(out_2[0, 4 * q : 4 * q + 4, :].bitcast(I32), y_s[32 * q : 32 * q + 4, :].bitcast(I32))
